import numpy as np
CORES = [3,5,43,45,51,53,67,69,75,77,83,85,91,93,115,117]
N = 16
GR, GC = 2, 8
L, KA, KB, F = 8, 1, 4, 128
def setup_inputs(rng):
    return {"a": rng.standard_normal((N, 128, KA * 128), dtype=np.float32), "b": rng.standard_normal((N, 128, KB * F), dtype=np.float32)}
def reference(a, b):
    A, B = a.astype(np.float64), b.astype(np.float64)
    y = np.zeros((N, 128, F))
    for i in range(GR):
        for j in range(GC):
            for k in range(L):
                At = A[i * GC + k // KA][:, 128 * (k % KA):128 * (k % KA) + 128]
                Bt = B[(k // KB) * GC + j][:, F * (k % KB):F * (k % KB) + F]
                y[i * GC + j] += At.T @ Bt
    return {"y": y.astype(np.float32 if a.dtype != np.float64 else np.float64)}

@@ -1,0 +1,182 @@
+from concourse.bass import DstId, RemoteDMATransfer
+
+NSIM = 128
+GC = 8
+KB = 4
+W = 128
+
+NOFF = 8
+NON = 8
+NH = 8
+HDIRECT = True
+RELAY_A = "helper"
+RELAY_B = "helper"
+
+SCRATCH = {
+    "A": ("sbuf", [128, 8 * W], "float32"),
+    "B": ("sbuf", [128, 8 * W], "float32"),
+    "S": ("sbuf", [128, KB * W], "float32"),
+    "o": ("sbuf", [128, W], "float32"),
+    "acc": ("psum", [128, W], "float32"),
+}
+SEMAPHORES = (["la", "lb", "snd", "mm", "cp", "st", "b0", "b1", "s0", "s1"] + ["a%d" % k for k in range(8)])
+
+
+def bits(m):
+    return [e for e in range(m.bit_length()) if (m >> e) & 1]
+
+
+def build(cores, topo):
+    rank_of = dict((c, r) for r, c in enumerate(cores))
+    calls, arr, est, bparts = {}, {}, {}, {}
+
+    def chipmates(c):
+        return [x for x in range(NSIM) if x != c and topo.chip(x) == topo.chip(c)]
+
+    def eng(c):
+        far = [x for x in cores if topo.chip(x) != topo.chip(c)][0]
+        off = bits(topo.mask(c, far))
+        hi = [e for e in bits(topo.mask(c, chipmates(c)[0])) if e not in off]
+        return off, hi
+
+    def tr(sb, sc, db, dc, w, to, sem, en, eta):
+        return dict(sb=sb, sc=sc, db=db, dc=dc, w=w, to=to, sem=sem, eng=en, eta=eta)
+
+    def send(src, t, waits, trs):
+        calls.setdefault(src, []).append((t, waits, trs))
+        for x in trs:
+            for n, d in enumerate(x["to"]):
+                arr[(d, x["sem"])] = arr.get((d, x["sem"]), 0) + len(x["eng"])
+                est[(d, x["sem"])] = x["eta"] + 0.7 * n
+
+    def forward(p, sec, sem, col, t):
+        if sec:
+            send(p, t, [sem], [tr("A", col, "A", col, W, sec, sem, eng(p)[1][:NON], t + 3.0)])
+
+    for r, c in enumerate(cores):
+        i, j = divmod(r, GC)
+        row = cores[i * GC:(i + 1) * GC]
+        partner = cores[(1 - i) * GC + j]
+        off, hi = eng(c)
+        peers = [p for p in row if p != c and topo.chip(p) == topo.chip(c)]
+        chips = []
+        for p in row:
+            if topo.chip(p) not in chips:
+                chips.append(topo.chip(p))
+        q = chips.index(topo.chip(c))
+        direct, cross = [], []
+        for s in range(1, len(chips)):
+            members = [p for p in row if topo.chip(p) == chips[(q + s) % len(chips)]]
+            prim = ([p for p in members if topo.die(p) == topo.die(c)] + members)[0]
+            sec = [p for p in members if p != prim]
+            (direct if topo.may_write(c, prim) else cross).append((prim, sec))
+        need = [p for p, s in cross] + ([] if topo.may_write(c, partner) else [partner])
+        helpers = [h for h in chipmates(c) if h not in rank_of and topo.die(h) == topo.die(c)
+                   and all(topo.may_write(h, x) for x in need)][:2]
+        prelay = [p for p in peers if all(topo.may_write(p, x) for x in need)][:1]
+        sa, col = "a%d" % j, j * W
+
+        ra = helpers if RELAY_A == "helper" else prelay
+        jobs = dict((h, cross[n::len(ra)]) for n, h in enumerate(ra))
+        on_to = [h for h in ra if jobs[h] and h not in peers] + peers
+        trs = [tr("A", col, "A", col, W, on_to, sa, hi[:NON], 5.0)]
+        if direct:
+            trs.append(tr("A", col, "A", col, W, [p for p, s in direct], sa, off[:NOFF], 5.5))
+        send(c, 2.0, ["la"], trs)
+        for n, (p, s) in enumerate(direct):
+            forward(p, s, sa, col, 5.5 + 0.7 * n)
+        for h in ra:
+            if jobs[h]:
+                to = []
+                for p, s in jobs[h]:
+                    to += [p] + (s if HDIRECT else [])
+                eta = 10.0 if h not in rank_of else 8.5
+                send(h, 5.0, [sa], [tr("A", col, "A", col, W, to, sa, eng(h)[0][:NH], eta)])
+                if not HDIRECT:
+                    for n, (p, s) in enumerate(jobs[h]):
+                        forward(p, s, sa, col, eta + 0.7 * n)
+
+        c0 = KB * i * W
+        if topo.may_write(c, partner):
+            send(c, 3.0, ["lb"], [tr("B", c0, "B", c0, KB * W, [partner], "b0", off[:NOFF], 9.0)])
+            bparts[partner] = 1
+        else:
+            rb = helpers if RELAY_B == "helper" else prelay
+            n_p = len(rb)
+            w = KB * W // n_p
+            alle = off + hi
+            ne = len(alle) // n_p
+            send(c, 3.0, ["lb"], [tr("B", c0 + n * w, "S", n * w, w, [h], "s%d" % n, alle[n * ne:(n + 1) * ne], 7.0)
+                                  for n, h in enumerate(rb)])
+            for n, h in enumerate(rb):
+                send(h, 7.0, ["s%d" % n], [tr("S", n * w, "B", c0 + n * w, w, [partner], "b%d" % n,
+                                              eng(h)[0][:NH], 12.0 + 0.5 * n)])
+            bparts[partner] = n_p
+    return calls, arr, est, bparts
+
+
+def rank_program(g, core, T, topo):
+    calls, arr, est, bparts = build(list(T.cores), topo)
+    rank = T.rank_of(core)
+    mine = sorted(calls.get(core, []), key=lambda x: x[0])
+    if rank is None and not mine:
+        return
+
+    def val(s):
+        return 16 if s in ("la", "lb") else arr[(core, s)]
+
+    if rank is not None:
+        i, j = divmod(rank, GC)
+        g.sync.dma_start(T.A[:, j * W:(j + 1) * W], T.a[:]).then_inc(T.sem.la, 16)
+        g.scalar.dma_start(T.B[:, KB * i * W:KB * (i + 1) * W], T.b[:]).then_inc(T.sem.lb, 16)
+
+    sent = 0
+    waited = set()
+    for t, waits, trs in mine:
+        for s in waits:
+            if s not in waited:
+                g.wait_ge(T.sem[s], val(s))
+                waited.add(s)
+        lst = []
+        for x in trs:
+            m = 0
+            for e in x["eng"]:
+                m |= 1 << e
+            ids = []
+            for d in x["to"]:
+                rid, pid, se = topo.addr(d)
+                ids.append(DstId(rid=rid, pnc=pid))
+            lst.append(RemoteDMATransfer(dst_ids=ids, dma_engine_mask=m, remote_sem=T.sem[x["sem"]],
+                                         srcs=[T[x["sb"]][:, x["sc"]:x["sc"] + x["w"]]],
+                                         dsts=[T[x["db"]][:, x["dc"]:x["dc"] + x["w"]] for d in x["to"]], alu_op=0))
+            sent += len(x["eng"])
+        g.remote_dma_fused(lst, local_sem=T.sem.snd)
+    if sent:
+        g.wait_ge(T.sem.snd, sent)
+    if rank is None:
+        return
+
+    prods = []
+    for k in range(8):
+        sa = "la" if k == j else "a%d" % k
+        if k // KB == i:
+            sb = "lb"
+        else:
+            sb = "b%d" % ((k % KB) * bparts[core] // KB)
+        ta = 2.0 if sa == "la" else est[(core, sa)]
+        tb = 3.0 if sb == "lb" else est[(core, sb)]
+        prods.append((max(ta, tb), k, sa, sb))
+    prods.sort()
+    seen = set()
+    for n, (t, k, sa, sb) in enumerate(prods):
+        for s in (sa, sb):
+            if s not in seen:
+                g.tensor.wait_ge(T.sem[s], val(s))
+                seen.add(s)
+        mmi = g.tensor.matmul(T.acc[:], T.A[:, k * W:(k + 1) * W], T.B[:, k * W:(k + 1) * W], n == 0, n == 7)
+    mmi.then_inc(T.sem.mm, 1)
+    g.vector.wait_ge(T.sem.mm, 1)
+    g.vector.tensor_copy(T.o[:], T.acc[:]).then_inc(T.sem.cp, 1)
+    g.sync.wait_ge(T.sem.cp, 1)
+    g.sync.dma_start(T.y[:], T.o[:]).then_inc(T.sem.st, 16)
+    g.sync.wait_ge(T.sem.st, 16)

@@ -8,7 +8,8 @@ W = 128
 NOFF = 8
 NON = 8
 NH = 8
-HDIRECT = True
+HDIRECT = False
+BSPLIT = True
 RELAY_A = "helper"
 RELAY_B = "helper"
 
@@ -98,8 +99,17 @@ def build(cores, topo):
 
         c0 = KB * i * W
         if topo.may_write(c, partner):
-            send(c, 3.0, ["lb"], [tr("B", c0, "B", c0, KB * W, [partner], "b0", off[:NOFF], 9.0)])
-            bparts[partner] = 1
+            hb = [h for h in chipmates(c) if h not in rank_of and topo.die(h) == topo.die(c)
+                  and topo.may_write(h, partner) and not jobs.get(h)]
+            if BSPLIT and hb:
+                w = KB * W // 2
+                send(c, 3.0, ["lb"], [tr("B", c0 + w, "S", w, w, hb[:1], "s1", hi[:NON], 6.0),
+                                      tr("B", c0, "B", c0, w, [partner], "b0", off[:NOFF], 8.0)])
+                send(hb[0], 6.0, ["s1"], [tr("S", w, "B", c0 + w, w, [partner], "b1", eng(hb[0])[0][:NH], 10.0)])
+                bparts[partner] = 2
+            else:
+                send(c, 3.0, ["lb"], [tr("B", c0, "B", c0, KB * W, [partner], "b0", off[:NOFF], 9.0)])
+                bparts[partner] = 1
         else:
             rb = helpers if RELAY_B == "helper" else prelay
             n_p = len(rb)

from concourse.bass import DstId, RemoteDMATransfer

NSIM = 128
GC = 8
KB = 4
W = 128

NOFF = 8
NON = 8
NH = 8
HDIRECT = False
BSPLIT = True
RELAY_A = "helper"
RELAY_B = "helper"

SCRATCH = {
    "A": ("sbuf", [128, 8 * W], "float32"),
    "B": ("sbuf", [128, 8 * W], "float32"),
    "S": ("sbuf", [128, KB * W], "float32"),
    "o": ("sbuf", [128, W], "float32"),
    "acc": ("psum", [128, W], "float32"),
}
SEMAPHORES = (["la", "lb", "snd", "mm", "cp", "st", "b0", "b1", "s0", "s1"] + ["a%d" % k for k in range(8)])


def bits(m):
    return [e for e in range(m.bit_length()) if (m >> e) & 1]


def build(cores, topo):
    rank_of = dict((c, r) for r, c in enumerate(cores))
    calls, arr, est, bparts = {}, {}, {}, {}

    def chipmates(c):
        return [x for x in range(NSIM) if x != c and topo.chip(x) == topo.chip(c)]

    def eng(c):
        far = [x for x in cores if topo.chip(x) != topo.chip(c)][0]
        off = bits(topo.mask(c, far))
        hi = [e for e in bits(topo.mask(c, chipmates(c)[0])) if e not in off]
        return off, hi

    def tr(sb, sc, db, dc, w, to, sem, en, eta):
        return dict(sb=sb, sc=sc, db=db, dc=dc, w=w, to=to, sem=sem, eng=en, eta=eta)

    def send(src, t, waits, trs):
        calls.setdefault(src, []).append((t, waits, trs))
        for x in trs:
            for n, d in enumerate(x["to"]):
                arr[(d, x["sem"])] = arr.get((d, x["sem"]), 0) + len(x["eng"])
                est[(d, x["sem"])] = x["eta"] + 0.7 * n

    def forward(p, sec, sem, col, t):
        if sec:
            send(p, t, [sem], [tr("A", col, "A", col, W, sec, sem, eng(p)[1][:NON], t + 3.0)])

    for r, c in enumerate(cores):
        i, j = divmod(r, GC)
        row = cores[i * GC:(i + 1) * GC]
        partner = cores[(1 - i) * GC + j]
        off, hi = eng(c)
        peers = [p for p in row if p != c and topo.chip(p) == topo.chip(c)]
        chips = []
        for p in row:
            if topo.chip(p) not in chips:
                chips.append(topo.chip(p))
        q = chips.index(topo.chip(c))
        direct, cross = [], []
        for s in range(1, len(chips)):
            members = [p for p in row if topo.chip(p) == chips[(q + s) % len(chips)]]
            prim = ([p for p in members if topo.die(p) == topo.die(c)] + members)[0]
            sec = [p for p in members if p != prim]
            (direct if topo.may_write(c, prim) else cross).append((prim, sec))
        need = [p for p, s in cross] + ([] if topo.may_write(c, partner) else [partner])
        helpers = [h for h in chipmates(c) if h not in rank_of and topo.die(h) == topo.die(c)
                   and all(topo.may_write(h, x) for x in need)][:2]
        prelay = [p for p in peers if all(topo.may_write(p, x) for x in need)][:1]
        sa, col = "a%d" % j, j * W

        ra = helpers if RELAY_A == "helper" else prelay
        jobs = dict((h, cross[n::len(ra)]) for n, h in enumerate(ra))
        on_to = [h for h in ra if jobs[h] and h not in peers] + peers
        trs = [tr("A", col, "A", col, W, on_to, sa, hi[:NON], 5.0)]
        if direct:
            trs.append(tr("A", col, "A", col, W, [p for p, s in direct], sa, off[:NOFF], 5.5))
        send(c, 2.0, ["la"], trs)
        for n, (p, s) in enumerate(direct):
            forward(p, s, sa, col, 5.5 + 0.7 * n)
        for h in ra:
            if jobs[h]:
                to = []
                for p, s in jobs[h]:
                    to += [p] + (s if HDIRECT else [])
                eta = 10.0 if h not in rank_of else 8.5
                send(h, 5.0, [sa], [tr("A", col, "A", col, W, to, sa, eng(h)[0][:NH], eta)])
                if not HDIRECT:
                    for n, (p, s) in enumerate(jobs[h]):
                        forward(p, s, sa, col, eta + 0.7 * n)

        c0 = KB * i * W
        if topo.may_write(c, partner):
            hb = [h for h in chipmates(c) if h not in rank_of and topo.die(h) == topo.die(c)
                  and topo.may_write(h, partner) and not jobs.get(h)]
            if BSPLIT and hb:
                w = KB * W // 2
                send(c, 3.0, ["lb"], [tr("B", c0 + w, "S", w, w, hb[:1], "s1", hi[:NON], 6.0),
                                      tr("B", c0, "B", c0, w, [partner], "b0", off[:NOFF], 8.0)])
                send(hb[0], 6.0, ["s1"], [tr("S", w, "B", c0 + w, w, [partner], "b1", eng(hb[0])[0][:NH], 10.0)])
                bparts[partner] = 2
            else:
                send(c, 3.0, ["lb"], [tr("B", c0, "B", c0, KB * W, [partner], "b0", off[:NOFF], 9.0)])
                bparts[partner] = 1
        else:
            rb = helpers if RELAY_B == "helper" else prelay
            n_p = len(rb)
            w = KB * W // n_p
            alle = off + hi
            ne = len(alle) // n_p
            send(c, 3.0, ["lb"], [tr("B", c0 + n * w, "S", n * w, w, [h], "s%d" % n, alle[n * ne:(n + 1) * ne], 7.0)
                                  for n, h in enumerate(rb)])
            for n, h in enumerate(rb):
                send(h, 7.0, ["s%d" % n], [tr("S", n * w, "B", c0 + n * w, w, [partner], "b%d" % n,
                                              eng(h)[0][:NH], 12.0 + 0.5 * n)])
            bparts[partner] = n_p
    return calls, arr, est, bparts


def rank_program(g, core, T, topo):
    calls, arr, est, bparts = build(list(T.cores), topo)
    rank = T.rank_of(core)
    mine = sorted(calls.get(core, []), key=lambda x: x[0])
    if rank is None and not mine:
        return

    def val(s):
        return 16 if s in ("la", "lb") else arr[(core, s)]

    if rank is not None:
        i, j = divmod(rank, GC)
        g.sync.dma_start(T.A[:, j * W:(j + 1) * W], T.a[:]).then_inc(T.sem.la, 16)
        g.scalar.dma_start(T.B[:, KB * i * W:KB * (i + 1) * W], T.b[:]).then_inc(T.sem.lb, 16)

    sent = 0
    waited = set()
    for t, waits, trs in mine:
        for s in waits:
            if s not in waited:
                g.wait_ge(T.sem[s], val(s))
                waited.add(s)
        lst = []
        for x in trs:
            m = 0
            for e in x["eng"]:
                m |= 1 << e
            ids = []
            for d in x["to"]:
                rid, pid, se = topo.addr(d)
                ids.append(DstId(rid=rid, pnc=pid))
            lst.append(RemoteDMATransfer(dst_ids=ids, dma_engine_mask=m, remote_sem=T.sem[x["sem"]],
                                         srcs=[T[x["sb"]][:, x["sc"]:x["sc"] + x["w"]]],
                                         dsts=[T[x["db"]][:, x["dc"]:x["dc"] + x["w"]] for d in x["to"]], alu_op=0))
            sent += len(x["eng"])
        g.remote_dma_fused(lst, local_sem=T.sem.snd)
    if sent:
        g.wait_ge(T.sem.snd, sent)
    if rank is None:
        return

    prods = []
    for k in range(8):
        sa = "la" if k == j else "a%d" % k
        if k // KB == i:
            sb = "lb"
        else:
            sb = "b%d" % ((k % KB) * bparts[core] // KB)
        ta = 2.0 if sa == "la" else est[(core, sa)]
        tb = 3.0 if sb == "lb" else est[(core, sb)]
        prods.append((max(ta, tb), k, sa, sb))
    prods.sort()
    seen = set()
    for n, (t, k, sa, sb) in enumerate(prods):
        for s in (sa, sb):
            if s not in seen:
                g.tensor.wait_ge(T.sem[s], val(s))
                seen.add(s)
        mmi = g.tensor.matmul(T.acc[:], T.A[:, k * W:(k + 1) * W], T.B[:, k * W:(k + 1) * W], n == 0, n == 7)
    mmi.then_inc(T.sem.mm, 1)
    g.vector.wait_ge(T.sem.mm, 1)
    g.vector.tensor_copy(T.o[:], T.acc[:]).then_inc(T.sem.cp, 1)
    g.sync.wait_ge(T.sem.cp, 1)
    g.sync.dma_start(T.y[:], T.o[:]).then_inc(T.sem.st, 16)
    g.sync.wait_ge(T.sem.st, 16)
